import numpy as np
import ml_dtypes


def mxq(x, axis, fmt="e4m3"):
    dtype, down = {"e4m3": (ml_dtypes.float8_e4m3fn, 7), "e5m2": (ml_dtypes.float8_e5m2, 14)}[fmt]
    v = np.moveaxis(np.asarray(x, np.float32).astype(ml_dtypes.bfloat16).astype(np.float64), axis, -1)
    blocks = v.reshape(v.shape[:-1] + (-1, 32))
    amax = np.abs(blocks).max(-1, keepdims=True)
    byte = np.maximum(np.where(amax > 0, np.frexp(amax)[1] - 1 + 127, 0) - down, 1)
    scale = np.exp2(byte - 127.0)
    codes = (blocks / scale).astype(np.float32).astype(dtype).astype(np.float64)
    return np.moveaxis((codes * scale).reshape(v.shape), -1, axis)


WIDE = False


def mx_kscale(k):
    if not WIDE:
        return np.ones(k)
    levels = np.array([10, -10, 5, -5, 0])
    if k % 512:
        return np.exp2(np.random.permutation(np.resize(levels, k // 32))).repeat(32)
    a = np.empty((k // 512, 16))
    for p in range(k // 512):
        a[p, :8] = np.random.permutation(np.resize(levels, 8))
        for g in range(8):
            far = levels[np.abs(levels - a[p, g]) >= 10]
            a[p, g + 8] = far[np.random.randint(len(far))]
    return np.exp2(a.ravel()).repeat(32)


def f64(x):
    return np.asarray(x).astype(np.float64)


def striped(idx):
    return np.tile(idx.reshape(-1, 16).T, (8, 1)).astype(np.uint16)


def unstriped(offs):
    return offs[:16].T.reshape(-1).astype(np.int64)


E2M1 = np.array([0.0, 0.5, 1.0, 1.5, 2.0, 3.0, 4.0, 6.0, -0.0, -0.5, -1.0, -1.5, -2.0, -3.0, -4.0, -6.0])


def pack_weight(w, fmt):
    k, n = w.shape
    w = f64(np.asarray(w, np.float32).astype(ml_dtypes.bfloat16)).reshape(k // 32, 32, n)
    amax = np.abs(w).max(1)
    if fmt == "e4m3":
        byte = np.frexp(amax)[1] - 1 + 127 - 7
    else:
        mant, ex = np.frexp(amax / 6.0)
        byte = np.where(mant > 0.5, ex, ex - 1) + 127
    byte = np.clip(np.where(amax > 0, byte, 1), 1, 254)
    scaled = (w * np.exp2(127.0 - byte)[:, None, :]).reshape(k, n).astype(np.float32)
    by_word = np.ascontiguousarray(scaled.reshape(k // 512, 128, 4, n).transpose(0, 1, 3, 2))
    if fmt == "e4m3":
        words = by_word.astype(ml_dtypes.float8_e4m3fn).view(np.uint8)
    else:
        c = by_word.astype(ml_dtypes.float4_e2m1fn).view(np.uint8) & 0xF
        words = (c[..., 0::2] | (c[..., 1::2] << 4)).reshape(k // 512, 128, 2 * n)
    return np.ascontiguousarray(words), np.ascontiguousarray(byte.astype(np.uint8).reshape(k // 512, 16, n))


def unpack_weight(words, scales, fmt):
    g, _, n = scales.shape
    words = np.ascontiguousarray(words).reshape(g, 128, n, -1)
    if fmt == "e4m3":
        vals = words.view(ml_dtypes.float8_e4m3fn).astype(np.float64)
    else:
        nib = np.empty((g, 128, n, 4), np.uint8)
        nib[..., 0::2] = words & 0xF
        nib[..., 1::2] = words >> 4
        vals = E2M1[nib]
    vals = vals * np.repeat(np.exp2(scales.astype(np.float64) - 127.0), 8, axis=1)[..., None]
    return vals.transpose(0, 1, 3, 2).reshape(g * 512, n)


def gelu(v):
    return 0.5 * v * (1.0 + np.tanh(np.sqrt(2.0 / np.pi) * (v + 0.044715 * v**3)))


K, R, H, T, S, T2, P = 1024, 512, 1024, 4096, 1024, 2048, 512

def setup_inputs():
    n = np.random.standard_normal
    s = mx_kscale(K)[:, None]
    u1 = mx_kscale(R)[:, None]
    u = mx_kscale(H)[:, None]
    d = {}
    d["tab_words"], d["tab_scales"] = pack_weight(n((K, T)) * s, "e4m3")
    d["offs"] = striped(np.random.permutation(T)[:S])
    d["w1"] = (n((K, R)) / K**0.5 / s * u1.T).astype(np.float32)
    d["w2_words"], d["w2_scales"] = pack_weight(n((K, R)) / K**0.5 / s * u1.T, "e2m1")
    d["w3"] = (n((R, H)) / R**0.5 / u1 * u.T).astype(np.float32)
    d["page0"] = (n((H, T2)) * u).astype(np.float32)
    d["wgs"] = np.exp(0.3 * n((128, S))).astype(np.float32)
    d["offs2"] = striped(np.random.permutation(T2)[:S])
    d["offs3"] = striped(np.random.permutation(T2)[:P])
    d["offs4"] = striped(np.random.permutation(T2)[:P])
    d["gs"] = (1.3 * np.exp(0.3 * n(H)) / u[:, 0]).astype(np.float32)
    d["gx"] = (1.3 * np.exp(0.3 * n(H)) * u[:, 0]).astype(np.float32)
    d["w4_words"], d["w4_scales"] = pack_weight(n((H, H)) / H**0.5 / u, "e4m3")
    d["gf"] = (np.exp(0.3 * n(H)) / u[:, 0]).astype(np.float32)
    return d

def reference(tab_words, tab_scales, offs, w1, w2_words, w2_scales, w3, page0, wgs, offs2, offs3, offs4, gs, gx, w4_words, w4_scales, gf):
    v = unpack_weight(tab_words, tab_scales, "e4m3")[:, unstriped(offs)]
    a = mxq(f64(w1), 0, "e4m3").T @ v
    b = unpack_weight(w2_words, w2_scales, "e2m1").T @ v
    low = np.minimum(a, b)
    h = mxq(f64(w3), 0, "e4m3").T @ mxq(low, 0, "e4m3")
    page = f64(page0).copy()
    page[:, unstriped(offs2)] = np.tile(f64(wgs), (H // 128, 1)) * h
    x = f64(gx)[:, None] * np.tanh(f64(gs)[:, None] * page[:, unstriped(offs3)])
    y = unpack_weight(w4_words, w4_scales, "e4m3").T @ mxq(x, 0, "e4m3")
    return np.tanh(y - f64(gf)[:, None] * page[:, unstriped(offs4)])

@@ -1,0 +1,315 @@
+from contextlib import ExitStack
+
+import concourse.mybir as mybir
+
+F32 = mybir.dt.float32
+BF16 = mybir.dt.bfloat16
+I32 = mybir.dt.int32
+U32 = mybir.dt.uint32
+U16 = mybir.dt.uint16
+U8 = mybir.dt.uint8
+FP8X4 = mybir.dt.float8_e4m3fn_x4
+FP4X4 = mybir.dt.float4_e2m1fn_x4
+ALU = mybir.AluOpType
+ACT = mybir.ActivationFunctionType
+
+K, R, H, T, S, T2, PICK = 1024, 512, 1024, 4096, 1024, 2048, 512
+FLOPS = 2 * (2 * K * R * S + R * H * S + H * H * PICK)
+
+P = 128
+KB = 1024
+
+
+def tile_list_vanilla_bundle_ledger_kernel(
+    tc, tab_words, tab_scales, offs, w1, w2_words, w2_scales, w3, page0, wgs,
+    offs2, offs3, offs4, gs, gx, w4_words, w4_scales, gf, out,
+):
+    nc = tc.nc
+    with ExitStack() as ctx:
+        held = ctx.enter_context(tc.tile_pool(name="held", bufs=1))
+        arena = ctx.enter_context(tc.tile_pool(name="arena", bufs=1))
+        psum = ctx.enter_context(tc.psum_pool(name="psum", bufs=1))
+
+        def keep(name, shape, dtype):
+            return held.tile(shape, dtype, name=name, align_bytes=64)
+
+        def place(name, shape, dtype, kib):
+            return arena.tile(shape, dtype, name=name, align_bytes=64, offset=kib * KB)
+
+        def bank(i):
+            return psum.tile([P, 512], F32, name="bank%d" % (i % 8))
+
+        list1 = keep("list1", [P, S // 16], U16)
+        list2 = keep("list2", [P, S // 16], U16)
+        list3 = keep("list3", [P, PICK // 16], U16)
+        list4 = keep("list4", [P, PICK // 16], U16)
+        tab_w = [place("tab_w%d" % a, [P, T], U32, 16 * a) for a in range(2)]
+        tab_s = keep("tab_s", [P, 2, T], U8)
+        s2_raw = keep("s2_raw", [P, 2, R], U8)
+        s4_raw = keep("s4_raw", [P, H], U8)
+
+        nc.vector.memset(tab_s[:].rearrange("p a c -> p (a c)").bitcast(I32), 0)
+        nc.gpsimd.memset(s2_raw[:].rearrange("p a c -> p (a c)").bitcast(I32), 0)
+        nc.gpsimd.memset(s4_raw[:].bitcast(I32), 0)
+
+
+        def load_table(a, pieces):
+            n = T // pieces
+            words = tab_words[a].rearrange("p n i -> p (n i)").bitcast(I32)
+            for e in range(pieces):
+                nc.sync.dma_start(out=tab_w[a][:, n * e : n * (e + 1)].bitcast(I32), in_=words[:, n * e : n * (e + 1)])
+
+        nc.sync.dma_start(list1[:], offs)
+        nc.sync.dma_start(list2[:], offs2)
+        nc.sync.dma_start(list3[:], offs3)
+        nc.sync.dma_start(list4[:], offs4)
+        load_table(0, 4)
+        for q in range(4):
+            nc.sync.dma_start(
+                out=tab_s[32 * q : 32 * q + 4, :, :].bitcast(I32),
+                in_=tab_scales[:, 4 * q : 4 * q + 4, :].bitcast(I32).rearrange("a r c -> r a c"),
+            )
+        for q in range(4):
+            nc.sync.dma_start(
+                out=s2_raw[32 * q : 32 * q + 4, :, :].bitcast(I32),
+                in_=w2_scales[:, 4 * q : 4 * q + 4, :].bitcast(I32).rearrange("a r c -> r a c"),
+            )
+        w2_raw = keep("w2_raw", [P, 2, 2 * R], U8)
+        nc.sync.dma_start(out=w2_raw[:].bitcast(I32), in_=w2_words.bitcast(I32).rearrange("a p c -> p a c"))
+        load_table(1, 1)
+
+        w1_rows = w1.rearrange("(a p i) m -> a p i m", a=2, i=4)
+        w1_raw0 = place("w1_raw0", [P, 4, R], F32, 32)
+        nc.sync.dma_start(out=w1_raw0[:], in_=w1_rows[0])
+        w1_raw1 = [place("w1_raw1_%d" % e, [P, 4, R // 2], F32, 40 + 4 * e) for e in range(2)]
+        for e in range(2):
+            nc.sync.dma_start(out=w1_raw1[e][:], in_=w1_rows[1][:, :, 256 * e : 256 * (e + 1)])
+
+        w3_rows = w3.rearrange("(p i) r -> p i r", i=4)
+        w3_raw = [place("w3_raw%d" % b, [P, 4, 512], F32, 72 + 8 * b) for b in range(2)]
+        nc.sync.dma_start(out=w3_raw[0][:], in_=w3_rows[:, :, 0:512])
+
+        wgs_rows = wgs.rearrange("(q t) j -> q t j", t=4)
+        wg_first = keep("wg_first", [P, S], F32)
+        wg_rest = keep("wg_rest", [P, 3, S], F32)
+        for q in range(4):
+            nc.sync.dma_start(out=wg_first[32 * q : 32 * q + 32, :], in_=wgs_rows[:, 0, :])
+        wg = [wg_first[:]] + [wg_rest[:, t, :] for t in range(3)]
+
+        page_rows = page0.rearrange("(b p t) c -> b t p c", b=2, t=4)
+        page = [keep("page%d" % i, [P, T2], F32) for i in range(8)]
+
+        def load_page(i):
+            nc.sync.dma_start(out=page[i][:], in_=page_rows[i // 4][i % 4])
+
+        def load_gain(name, vec):
+            tile = keep(name, [P, 8], F32)
+            nc.sync.dma_start(
+                out=tile[:].rearrange("p (b t) -> p b t", t=4),
+                in_=vec.rearrange("(b p t) -> p b t", b=2, t=4),
+            )
+            return tile
+
+        load_page(0)
+        nc.sync.dma_start(out=w3_raw[1][:], in_=w3_rows[:, :, 512:1024])
+        gs_sb = load_gain("gs_sb", gs)
+        gx_sb = load_gain("gx_sb", gx)
+        for q in range(4):
+            nc.sync.dma_start(out=wg_rest[32 * q : 32 * q + 32, :, :], in_=wgs_rows[:, 1:4, :])
+        load_page(1)
+        w4_raw = keep("w4_raw", [P, 2, H], U32)
+        nc.sync.dma_start(
+            out=w4_raw[:].bitcast(I32),
+            in_=w4_words.rearrange("a p c i -> p a (c i)").bitcast(I32),
+        )
+        gf_sb = load_gain("gf_sb", gf)
+        for q in range(4):
+            nc.sync.dma_start(
+                out=s4_raw[32 * q : 32 * q + 8, :].bitcast(I32),
+                in_=w4_scales[:, 4 * q : 4 * q + 4, :].bitcast(I32),
+            )
+        for i in range(2, 8):
+            load_page(i)
+
+        v_s = [keep("v_s%d" % a, [P, S], U8) for a in range(2)]
+        v_w = [keep("v_w%d" % a, [P, S], U32) for a in range(2)]
+        nc.vector.tensor_copy(v_w[0][:], tab_w[0][:].indirect(list1[:]))
+        for a in range(2):
+            nc.vector.tensor_copy(v_s[a][:], tab_s[:, a, :].indirect(list1[:]))
+
+        w2_w = keep("w2_w", [P, 2, 2 * R], U8)
+        nc.scalar.copy(
+            out=w2_w[:].bitcast(U16).rearrange("p a (u c) -> p a u c", u=4),
+            in_=w2_raw[:].bitcast(U16).rearrange("p a (c u) -> p a u c", u=4),
+        )
+        w2_s = keep("w2_s", [P, 2, R], U8)
+        nc.vector.tensor_copy(
+            out=w2_s[:].rearrange("p a (u c) -> p a u c", u=4),
+            in_=s2_raw[:].rearrange("p a (c u) -> p a u c", u=4),
+        )
+        for g in range(4):
+            nc.vector.tensor_copy(v_w[1][:, 256 * g : 256 * (g + 1)], tab_w[1][:].indirect(list1[:, 16 * g : 16 * (g + 1)]))
+
+        def first_stage(acc, c, words, scales):
+            cols = slice(128 * c, 128 * (c + 1))
+            for a in range(2):
+                for u in range(4):
+                    nc.tensor.matmul_mx(
+                        out=acc[:, 128 * u : 128 * (u + 1)],
+                        lhsT=words(a, u),
+                        lhsT_scale=scales(a, u),
+                        rhs=v_w[a][:, cols].bitcast(FP8X4),
+                        rhs_scale=v_s[a][:, cols],
+                        start=(a == 0 and u == 0),
+                        stop=(a == 1 and u == 3),
+                    )
+
+        b_sb = [place("b_sb%d" % c, [P, 128, 4], F32, 48 + 2 * c) for c in range(8)]
+        for c in range(8):
+            acc = bank(c)
+            first_stage(
+                acc, c,
+                lambda a, u: w2_w[:, a, 256 * u : 256 * (u + 1)].bitcast(FP4X4),
+                lambda a, u: w2_s[:, a, 128 * u : 128 * (u + 1)],
+            )
+            nc.scalar.copy(out=b_sb[c][:], in_=acc[:].rearrange("p (u n) -> p n u", u=4))
+
+        w1_bf = [place("w1_bf%d" % a, [P, 4, 128, 4], BF16, 64 + 4 * a) for a in range(2)]
+        w1_w = keep("w1_w", [P, 2, R], U32)
+        w1_s = keep("w1_s", [P, 2, R], U8)
+
+        def quantize(words, scales, values):
+            nc.vector.quantize_mx(out=words.bitcast(FP8X4), scales=scales, in_=values)
+
+        nc.vector.tensor_copy(
+            out=w1_bf[0][:].rearrange("p u c i -> p c u i"),
+            in_=w1_raw0[:].rearrange("p i (c u) -> p c u i", u=4),
+        )
+        quantize(w1_w[:, 0, :], w1_s[:, 0, :], w1_bf[0][:].rearrange("p u c i -> p (u c i)"))
+        for e in range(2):
+            nc.vector.tensor_copy(
+                out=w1_bf[1][:, :, 64 * e : 64 * (e + 1), :].rearrange("p u c i -> p c u i"),
+                in_=w1_raw1[e][:].rearrange("p i (c u) -> p c u i", u=4),
+            )
+        quantize(w1_w[:, 1, :], w1_s[:, 1, :], w1_bf[1][:].rearrange("p u c i -> p (u c i)"))
+
+        low_bf = [place("low_bf%d" % e, [P, 512, 4], BF16, 32 + 4 * e) for e in range(2)]
+        low_w = keep("low_w", [P, S], U32)
+        low_s = keep("low_s", [P, S], U8)
+        w3_bf = [place("w3_bf%d" % b, [P, 4, 128, 4], BF16, 88 + 4 * b) for b in range(2)]
+        w3_w = keep("w3_w", [P, H], U32)
+        w3_s = keep("w3_s", [P, H], U8)
+
+        def prepare_w3(b):
+            nc.scalar.copy(
+                out=w3_bf[b][:].rearrange("p u c i -> p c u i"),
+                in_=w3_raw[b][:].rearrange("p i (c u) -> p c u i", u=4),
+            )
+            cols = slice(512 * b, 512 * (b + 1))
+            quantize(w3_w[:, cols], w3_s[:, cols], w3_bf[b][:].rearrange("p u c i -> p (u c i)"))
+
+        prepare_w3(0)
+        for c in range(8):
+            acc = bank(c)
+            first_stage(
+                acc, c,
+                lambda a, u: w1_w[:, a, 128 * u : 128 * (u + 1)].bitcast(FP8X4),
+                lambda a, u: w1_s[:, a, 128 * u : 128 * (u + 1)],
+            )
+            e, n0 = c // 4, 128 * (c % 4)
+            nc.vector.tensor_tensor(
+                low_bf[e][:, n0 : n0 + 128, :], acc[:].rearrange("p (u n) -> p n u", u=4), b_sb[c][:], ALU.min
+            )
+            if c % 4 == 3:
+                cols = slice(512 * e, 512 * (e + 1))
+                quantize(low_w[:, cols], low_s[:, cols], low_bf[e][:].rearrange("p n u -> p (n u)"))
+        prepare_w3(1)
+
+        h_sb = [place("h_sb%d" % i, [P, S], F32, 4 * i) for i in range(8)]
+        for i in range(8):
+            rows = slice(128 * i, 128 * (i + 1))
+            for e in range(2):
+                cols = slice(512 * e, 512 * (e + 1))
+                acc = bank(2 * i + e)
+                nc.tensor.matmul_mx(
+                    out=acc[:],
+                    lhsT=w3_w[:, rows].bitcast(FP8X4),
+                    lhsT_scale=w3_s[:, rows],
+                    rhs=low_w[:, cols].bitcast(FP8X4),
+                    rhs_scale=low_s[:, cols],
+                    start=True,
+                    stop=True,
+                )
+                nc.scalar.copy(out=h_sb[i][:, cols], in_=acc[:])
+
+        w4_w = place("w4_w", [P, 2, H], U32, 64)
+        for a in range(2):
+            nc.scalar.copy(
+                out=w4_w[:, a, :].rearrange("p (b u c) -> p b c u", b=2, u=4),
+                in_=w4_raw[:, a, :].rearrange("p (b c u) -> p b c u", b=2, u=4),
+            )
+
+        w4_s = keep("w4_s", [P, H], U8)
+        nc.vector.tensor_copy(
+            out=w4_s[:].rearrange("p (b u c) -> p b u c", b=2, u=4),
+            in_=s4_raw[:].rearrange("p (b c u) -> p b u c", b=2, u=4),
+        )
+        x_bf = [place("x_bf%d" % b, [P, PICK, 4], BF16, 88 + 4 * b) for b in range(2)]
+        x_w = keep("x_w", [P, 2, PICK], U32)
+        x_s = keep("x_s", [P, 2, PICK], U8)
+        z_at = [32, 34, 36, 38, 28, 30, 92, 94]
+        z = {}
+        y = {}
+
+        def fetch_finished(i):
+            z[i] = place("z%d" % i, [P, PICK], F32, z_at[i])
+            nc.vector.tensor_copy(z[i][:], page[i][:].indirect(list4[:]))
+
+        def second_stage(a):
+            for i in range(8):
+                if a == 0:
+                    y[i] = bank(i)
+                rows = slice(128 * i, 128 * (i + 1))
+                nc.tensor.matmul_mx(
+                    out=y[i][:],
+                    lhsT=w4_w[:, a, rows].bitcast(FP8X4),
+                    lhsT_scale=w4_s[4 * a : P, rows],
+                    rhs=x_w[:, a, :].bitcast(FP8X4),
+                    rhs_scale=x_s[:, a, :],
+                    start=(a == 0),
+                    stop=(a == 1),
+                )
+
+        for i in range(8):
+            b, t = divmod(i, 4)
+            pieces = 2 if i == 0 else 1
+            n = S // pieces
+            for e in range(pieces):
+                cols = slice(n * e, n * (e + 1))
+                nc.vector.tensor_tensor(
+                    page[i][:].indirect(list2[:, n // 16 * e : n // 16 * (e + 1)]),
+                    h_sb[i][:, cols], wg[t][:, cols], ALU.mult,
+                )
+            picked = place("picked%d" % i, [P, PICK], F32, 72 + 2 * (i % 4))
+            nc.vector.tensor_copy(picked[:], page[i][:].indirect(list3[:]))
+            bent = place("bent%d" % i, [P, PICK], F32, 80 + 2 * (i % 4))
+            nc.scalar.activation(bent[:], picked[:], ACT.Tanh, scale=gs_sb[:, i : i + 1])
+            nc.scalar.activation(x_bf[b][:, :, t], bent[:], ACT.Copy, scale=gx_sb[:, i : i + 1])
+            if i < 4:
+                fetch_finished(i)
+            if i == 7:
+                fetch_finished(4)
+                fetch_finished(5)
+            if t == 3:
+                quantize(x_w[:, b, :], x_s[:, b, :], x_bf[b][:].rearrange("p n t -> p (n t)"))
+                second_stage(b)
+        fetch_finished(6)
+        fetch_finished(7)
+
+        out_rows = out.rearrange("(b p t) j -> b t p j", b=2, t=4)
+        for i in range(8):
+            diff = place("diff%d" % i, [P, PICK], F32, 40 + 2 * (i % 4))
+            nc.vector.scalar_tensor_tensor(diff[:], z[i][:], gf_sb[:, i : i + 1], y[i][:], ALU.mult, ALU.subtract)
+            res = place("res%d" % i, [P, PICK], F32, 48 + 2 * i)
+            nc.scalar.activation(res[:], diff[:], ACT.Tanh, scale=-1.0)
+            nc.sync.dma_start(out=out_rows[i // 4][i % 4], in_=res[:])

@@ -44,31 +44,31 @@ def tile_list_vanilla_bundle_ledger_kernel(
         list3 = keep("list3", [P, PICK // 16], U16)
         list4 = keep("list4", [P, PICK // 16], U16)
         tab_w = [place("tab_w%d" % a, [P, T], U32, 16 * a) for a in range(2)]
-        tab_s = keep("tab_s", [P, 2, T], U8)
+        tab_s = keep("tab_s", [P, T], U8)
+        v_s = [keep("v_s%d" % a, [P, S], U8) for a in range(2)]
         s2_raw = keep("s2_raw", [P, 2, R], U8)
         s4_raw = keep("s4_raw", [P, H], U8)
 
-        nc.vector.memset(tab_s[:].rearrange("p a c -> p (a c)").bitcast(I32), 0)
+        nc.vector.memset(tab_s[:].bitcast(I32), 0)
+        nc.gpsimd.memset(v_s[1][:].bitcast(I32), 0)
         nc.gpsimd.memset(s2_raw[:].rearrange("p a c -> p (a c)").bitcast(I32), 0)
         nc.gpsimd.memset(s4_raw[:].bitcast(I32), 0)
 
 
-        def load_table(a, pieces):
-            n = T // pieces
+        def load_table(a, first, last, n):
             words = tab_words[a].rearrange("p n i -> p (n i)").bitcast(I32)
-            for e in range(pieces):
-                nc.sync.dma_start(out=tab_w[a][:, n * e : n * (e + 1)].bitcast(I32), in_=words[:, n * e : n * (e + 1)])
+            for c in range(first, last, n):
+                nc.sync.dma_start(out=tab_w[a][:, c : c + n].bitcast(I32), in_=words[:, c : c + n])
 
         nc.sync.dma_start(list1[:], offs)
         nc.sync.dma_start(list2[:], offs2)
         nc.sync.dma_start(list3[:], offs3)
         nc.sync.dma_start(list4[:], offs4)
-        load_table(0, 4)
-        for q in range(4):
-            nc.sync.dma_start(
-                out=tab_s[32 * q : 32 * q + 4, :, :].bitcast(I32),
-                in_=tab_scales[:, 4 * q : 4 * q + 4, :].bitcast(I32).rearrange("a r c -> r a c"),
-            )
+        load_table(0, 0, 2048, 512)
+        tab_rows = tab_scales.bitcast(I32).rearrange("a (q r) n -> r q a n", r=4)
+        for r in range(4):
+            nc.sync.dma_start(out=tab_s[r:P:16, :].bitcast(I32), in_=tab_rows[r])
+        load_table(0, 2048, T, 1024)
         for q in range(4):
             nc.sync.dma_start(
                 out=s2_raw[32 * q : 32 * q + 4, :, :].bitcast(I32),
@@ -76,7 +76,9 @@ def tile_list_vanilla_bundle_ledger_kernel(
             )
         w2_raw = keep("w2_raw", [P, 2, 2 * R], U8)
         nc.sync.dma_start(out=w2_raw[:].bitcast(I32), in_=w2_words.bitcast(I32).rearrange("a p c -> p a c"))
-        load_table(1, 1)
+        load_table(1, 0, T, T)
+        nc.vector.tensor_copy(v_s[0][:], tab_s[:].indirect(list1[:]))
+        nc.sync.dma_start(out=v_s[1][0:112, :].bitcast(I32), in_=v_s[0][16:128, :].bitcast(I32))
 
         w1_rows = w1.rearrange("(a p i) m -> a p i m", a=2, i=4)
         w1_raw0 = place("w1_raw0", [P, 4, R], F32, 32)
@@ -85,9 +87,14 @@ def tile_list_vanilla_bundle_ledger_kernel(
         for e in range(2):
             nc.sync.dma_start(out=w1_raw1[e][:], in_=w1_rows[1][:, :, 256 * e : 256 * (e + 1)])
 
-        w3_rows = w3.rearrange("(p i) r -> p i r", i=4)
+        w3_rows = w3.rearrange("(g i q) r -> i g q r", i=4, q=8)
         w3_raw = [place("w3_raw%d" % b, [P, 4, 512], F32, 72 + 8 * b) for b in range(2)]
-        nc.sync.dma_start(out=w3_raw[0][:], in_=w3_rows[:, :, 0:512])
+
+        def load_w3(b):
+            for i in range(4):
+                nc.sync.dma_start(out=w3_raw[b][:, i, :], in_=w3_rows[i][:, :, 512 * b : 512 * (b + 1)])
+
+        load_w3(0)
 
         wgs_rows = wgs.rearrange("(q t) j -> q t j", t=4)
         wg_first = keep("wg_first", [P, S], F32)
@@ -111,7 +118,7 @@ def tile_list_vanilla_bundle_ledger_kernel(
             return tile
 
         load_page(0)
-        nc.sync.dma_start(out=w3_raw[1][:], in_=w3_rows[:, :, 512:1024])
+        load_w3(1)
         gs_sb = load_gain("gs_sb", gs)
         gx_sb = load_gain("gx_sb", gx)
         for q in range(4):
@@ -131,21 +138,18 @@ def tile_list_vanilla_bundle_ledger_kernel(
         for i in range(2, 8):
             load_page(i)
 
-        v_s = [keep("v_s%d" % a, [P, S], U8) for a in range(2)]
         v_w = [keep("v_w%d" % a, [P, S], U32) for a in range(2)]
         nc.vector.tensor_copy(v_w[0][:], tab_w[0][:].indirect(list1[:]))
-        for a in range(2):
-            nc.vector.tensor_copy(v_s[a][:], tab_s[:, a, :].indirect(list1[:]))
 
         w2_w = keep("w2_w", [P, 2, 2 * R], U8)
         nc.scalar.copy(
-            out=w2_w[:].bitcast(U16).rearrange("p a (u c) -> p a u c", u=4),
-            in_=w2_raw[:].bitcast(U16).rearrange("p a (c u) -> p a u c", u=4),
+            out=w2_w[:].bitcast(U32).rearrange("p a (u g w) -> p a u g w", u=4, g=16),
+            in_=w2_raw[:].bitcast(U32).rearrange("p a (g u w) -> p a u g w", u=4, g=16),
         )
         w2_s = keep("w2_s", [P, 2, R], U8)
-        nc.vector.tensor_copy(
-            out=w2_s[:].rearrange("p a (u c) -> p a u c", u=4),
-            in_=s2_raw[:].rearrange("p a (c u) -> p a u c", u=4),
+        nc.scalar.copy(
+            out=w2_s[:].bitcast(U32).rearrange("p a (u g w) -> p a u g w", u=4, g=16),
+            in_=s2_raw[:].bitcast(U32).rearrange("p a (g u w) -> p a u g w", u=4, g=16),
         )
         for g in range(4):
             nc.vector.tensor_copy(v_w[1][:, 256 * g : 256 * (g + 1)], tab_w[1][:].indirect(list1[:, 16 * g : 16 * (g + 1)]))
@@ -182,14 +186,14 @@ def tile_list_vanilla_bundle_ledger_kernel(
             nc.vector.quantize_mx(out=words.bitcast(FP8X4), scales=scales, in_=values)
 
         nc.vector.tensor_copy(
-            out=w1_bf[0][:].rearrange("p u c i -> p c u i"),
-            in_=w1_raw0[:].rearrange("p i (c u) -> p c u i", u=4),
+            out=w1_bf[0][:].rearrange("p u (g q) i -> p u g q i", q=8),
+            in_=w1_raw0[:].rearrange("p i (g u q) -> p u g q i", u=4, q=8),
         )
         quantize(w1_w[:, 0, :], w1_s[:, 0, :], w1_bf[0][:].rearrange("p u c i -> p (u c i)"))
         for e in range(2):
             nc.vector.tensor_copy(
-                out=w1_bf[1][:, :, 64 * e : 64 * (e + 1), :].rearrange("p u c i -> p c u i"),
-                in_=w1_raw1[e][:].rearrange("p i (c u) -> p c u i", u=4),
+                out=w1_bf[1][:, :, 64 * e : 64 * (e + 1), :].rearrange("p u (g q) i -> p u g q i", q=8),
+                in_=w1_raw1[e][:].rearrange("p i (g u q) -> p u g q i", u=4, q=8),
             )
         quantize(w1_w[:, 1, :], w1_s[:, 1, :], w1_bf[1][:].rearrange("p u c i -> p (u c i)"))
 

@@ -50,10 +50,15 @@ def tile_list_vanilla_bundle_ledger_kernel(
         s4_raw = keep("s4_raw", [P, H], U8)
 
         nc.vector.memset(tab_s[:].bitcast(I32), 0)
-        nc.gpsimd.memset(v_s[1][:].bitcast(I32), 0)
         nc.gpsimd.memset(s2_raw[:].rearrange("p a c -> p (a c)").bitcast(I32), 0)
-        nc.gpsimd.memset(s4_raw[:].bitcast(I32), 0)
+        nc.vector.memset(v_s[1][:].bitcast(I32), 0)
+        nc.vector.memset(s4_raw[:].bitcast(I32), 0)
 
+        for q in range(4):
+            nc.gpsimd.dma_start(
+                out=s2_raw[32 * q : 32 * q + 4, :, :].bitcast(I32),
+                in_=w2_scales[:, 4 * q : 4 * q + 4, :].bitcast(I32).rearrange("a r c -> r a c"),
+            )
 
         def load_table(a, first, last, n):
             words = tab_words[a].rearrange("p n i -> p (n i)").bitcast(I32)
@@ -61,24 +66,14 @@ def tile_list_vanilla_bundle_ledger_kernel(
                 nc.sync.dma_start(out=tab_w[a][:, c : c + n].bitcast(I32), in_=words[:, c : c + n])
 
         nc.sync.dma_start(list1[:], offs)
-        nc.sync.dma_start(list2[:], offs2)
-        nc.sync.dma_start(list3[:], offs3)
-        nc.sync.dma_start(list4[:], offs4)
-        load_table(0, 0, 2048, 512)
+        load_table(0, 0, T - 512, 512)
         tab_rows = tab_scales.bitcast(I32).rearrange("a (q r) n -> r q a n", r=4)
         for r in range(4):
             nc.sync.dma_start(out=tab_s[r:P:16, :].bitcast(I32), in_=tab_rows[r])
-        load_table(0, 2048, T, 1024)
-        for q in range(4):
-            nc.sync.dma_start(
-                out=s2_raw[32 * q : 32 * q + 4, :, :].bitcast(I32),
-                in_=w2_scales[:, 4 * q : 4 * q + 4, :].bitcast(I32).rearrange("a r c -> r a c"),
-            )
+        load_table(0, T - 512, T, 512)
         w2_raw = keep("w2_raw", [P, 2, 2 * R], U8)
         nc.sync.dma_start(out=w2_raw[:].bitcast(I32), in_=w2_words.bitcast(I32).rearrange("a p c -> p a c"))
         load_table(1, 0, T, T)
-        nc.vector.tensor_copy(v_s[0][:], tab_s[:].indirect(list1[:]))
-        nc.sync.dma_start(out=v_s[1][0:112, :].bitcast(I32), in_=v_s[0][16:128, :].bitcast(I32))
 
         w1_rows = w1.rearrange("(a p i) m -> a p i m", a=2, i=4)
         w1_raw0 = place("w1_raw0", [P, 4, R], F32, 32)
@@ -87,21 +82,18 @@ def tile_list_vanilla_bundle_ledger_kernel(
         for e in range(2):
             nc.sync.dma_start(out=w1_raw1[e][:], in_=w1_rows[1][:, :, 256 * e : 256 * (e + 1)])
 
-        w3_rows = w3.rearrange("(g i q) r -> i g q r", i=4, q=8)
+        w3_rows = w3.rearrange("(p i) r -> p i r", i=4)
         w3_raw = [place("w3_raw%d" % b, [P, 4, 512], F32, 72 + 8 * b) for b in range(2)]
 
         def load_w3(b):
-            for i in range(4):
-                nc.sync.dma_start(out=w3_raw[b][:, i, :], in_=w3_rows[i][:, :, 512 * b : 512 * (b + 1)])
-
-        load_w3(0)
+            nc.sync.dma_start(out=w3_raw[b][:], in_=w3_rows[:, :, 512 * b : 512 * (b + 1)])
 
         wgs_rows = wgs.rearrange("(q t) j -> q t j", t=4)
-        wg_first = keep("wg_first", [P, S], F32)
-        wg_rest = keep("wg_rest", [P, 3, S], F32)
-        for q in range(4):
-            nc.sync.dma_start(out=wg_first[32 * q : 32 * q + 32, :], in_=wgs_rows[:, 0, :])
-        wg = [wg_first[:]] + [wg_rest[:, t, :] for t in range(3)]
+        wg = [keep("wg%d" % t, [P, S], F32) for t in range(4)]
+
+        def load_wg(t, cols):
+            for q in (0, 2, 1, 3):
+                nc.sync.dma_start(out=wg[t][32 * q : 32 * q + 32, cols], in_=wgs_rows[:, t, cols])
 
         page_rows = page0.rearrange("(b p t) c -> b t p c", b=2, t=4)
         page = [keep("page%d" % i, [P, T2], F32) for i in range(8)]
@@ -117,39 +109,51 @@ def tile_list_vanilla_bundle_ledger_kernel(
             )
             return tile
 
+        load_w3(0)
+        load_wg(0, slice(0, 512))
+        nc.sync.dma_start(list2[:], offs2)
         load_page(0)
-        load_w3(1)
+        load_wg(0, slice(512, S))
+        nc.sync.dma_start(list3[:], offs3)
+        nc.sync.dma_start(list4[:], offs4)
+        load_wg(1, slice(0, S))
+        load_page(1)
         gs_sb = load_gain("gs_sb", gs)
         gx_sb = load_gain("gx_sb", gx)
-        for q in range(4):
-            nc.sync.dma_start(out=wg_rest[32 * q : 32 * q + 32, :, :], in_=wgs_rows[:, 1:4, :])
-        load_page(1)
+        load_wg(2, slice(0, S))
+        load_page(2)
+        load_w3(1)
+        load_wg(3, slice(0, S))
+        load_page(3)
         w4_raw = keep("w4_raw", [P, 2, H], U32)
         nc.sync.dma_start(
             out=w4_raw[:].bitcast(I32),
             in_=w4_words.rearrange("a p c i -> p a (c i)").bitcast(I32),
         )
+        load_page(4)
         gf_sb = load_gain("gf_sb", gf)
         for q in range(4):
             nc.sync.dma_start(
                 out=s4_raw[32 * q : 32 * q + 8, :].bitcast(I32),
                 in_=w4_scales[:, 4 * q : 4 * q + 4, :].bitcast(I32),
             )
-        for i in range(2, 8):
+        for i in range(5, 8):
             load_page(i)
 
+        nc.vector.tensor_copy(v_s[0][:], tab_s[:].indirect(list1[:]))
+        nc.gpsimd.dma_start(out=v_s[1][0:112, :].bitcast(I32), in_=v_s[0][16:128, :].bitcast(I32))
         v_w = [keep("v_w%d" % a, [P, S], U32) for a in range(2)]
         nc.vector.tensor_copy(v_w[0][:], tab_w[0][:].indirect(list1[:]))
 
         w2_w = keep("w2_w", [P, 2, 2 * R], U8)
         nc.scalar.copy(
-            out=w2_w[:].bitcast(U32).rearrange("p a (u g w) -> p a u g w", u=4, g=16),
-            in_=w2_raw[:].bitcast(U32).rearrange("p a (g u w) -> p a u g w", u=4, g=16),
+            out=w2_w[:].bitcast(U16).rearrange("p a (u c) -> p a u c", u=4),
+            in_=w2_raw[:].bitcast(U16).rearrange("p a (c u) -> p a u c", u=4),
         )
-        w2_s = keep("w2_s", [P, 2, R], U8)
-        nc.scalar.copy(
-            out=w2_s[:].bitcast(U32).rearrange("p a (u g w) -> p a u g w", u=4, g=16),
-            in_=s2_raw[:].bitcast(U32).rearrange("p a (g u w) -> p a u g w", u=4, g=16),
+        w2_s = place("w2_s", [P, 2, R], U8, 12)
+        nc.vector.tensor_copy(
+            out=w2_s[:].rearrange("p a (u c) -> p a u c", u=4),
+            in_=s2_raw[:].rearrange("p a (c u) -> p a u c", u=4),
         )
         for g in range(4):
             nc.vector.tensor_copy(v_w[1][:, 256 * g : 256 * (g + 1)], tab_w[1][:].indirect(list1[:, 16 * g : 16 * (g + 1)]))
@@ -186,14 +190,14 @@ def tile_list_vanilla_bundle_ledger_kernel(
             nc.vector.quantize_mx(out=words.bitcast(FP8X4), scales=scales, in_=values)
 
         nc.vector.tensor_copy(
-            out=w1_bf[0][:].rearrange("p u (g q) i -> p u g q i", q=8),
-            in_=w1_raw0[:].rearrange("p i (g u q) -> p u g q i", u=4, q=8),
+            out=w1_bf[0][:].rearrange("p u c i -> p c u i"),
+            in_=w1_raw0[:].rearrange("p i (c u) -> p c u i", u=4),
         )
         quantize(w1_w[:, 0, :], w1_s[:, 0, :], w1_bf[0][:].rearrange("p u c i -> p (u c i)"))
         for e in range(2):
             nc.vector.tensor_copy(
-                out=w1_bf[1][:, :, 64 * e : 64 * (e + 1), :].rearrange("p u (g q) i -> p u g q i", q=8),
-                in_=w1_raw1[e][:].rearrange("p i (g u q) -> p u g q i", u=4, q=8),
+                out=w1_bf[1][:, :, 64 * e : 64 * (e + 1), :].rearrange("p u c i -> p c u i"),
+                in_=w1_raw1[e][:].rearrange("p i (c u) -> p c u i", u=4),
             )
         quantize(w1_w[:, 1, :], w1_s[:, 1, :], w1_bf[1][:].rearrange("p u c i -> p (u c i)"))
 

@@ -44,20 +44,25 @@ def tile_list_vanilla_bundle_ledger_kernel(
         list3 = keep("list3", [P, PICK // 16], U16)
         list4 = keep("list4", [P, PICK // 16], U16)
         tab_w = [place("tab_w%d" % a, [P, T], U32, 16 * a) for a in range(2)]
-        tab_s = keep("tab_s", [P, T], U8)
+        tab_s = place("tab_s", [P, T], U8, 104)
         v_s = [keep("v_s%d" % a, [P, S], U8) for a in range(2)]
         s2_raw = keep("s2_raw", [P, 2, R], U8)
         s4_raw = keep("s4_raw", [P, H], U8)
 
         nc.vector.memset(tab_s[:].bitcast(I32), 0)
         nc.gpsimd.memset(s2_raw[:].rearrange("p a c -> p (a c)").bitcast(I32), 0)
-        nc.vector.memset(v_s[1][:].bitcast(I32), 0)
         nc.vector.memset(s4_raw[:].bitcast(I32), 0)
+        nc.vector.memset(v_s[1][:].bitcast(I32), 0)
 
         for q in range(4):
             nc.gpsimd.dma_start(
                 out=s2_raw[32 * q : 32 * q + 4, :, :].bitcast(I32),
                 in_=w2_scales[:, 4 * q : 4 * q + 4, :].bitcast(I32).rearrange("a r c -> r a c"),
+            )
+        for q in range(4):
+            nc.gpsimd.dma_start(
+                out=s4_raw[32 * q : 32 * q + 8, :].bitcast(I32),
+                in_=w4_scales[:, 4 * q : 4 * q + 4, :].bitcast(I32),
             )
 
         def load_table(a, first, last, n):
@@ -76,11 +81,9 @@ def tile_list_vanilla_bundle_ledger_kernel(
         load_table(1, 0, T, T)
 
         w1_rows = w1.rearrange("(a p i) m -> a p i m", a=2, i=4)
-        w1_raw0 = place("w1_raw0", [P, 4, R], F32, 32)
-        nc.sync.dma_start(out=w1_raw0[:], in_=w1_rows[0])
-        w1_raw1 = [place("w1_raw1_%d" % e, [P, 4, R // 2], F32, 40 + 4 * e) for e in range(2)]
-        for e in range(2):
-            nc.sync.dma_start(out=w1_raw1[e][:], in_=w1_rows[1][:, :, 256 * e : 256 * (e + 1)])
+        w1_raw = [place("w1_raw%d" % a, [P, 4, R], F32, 32 + 8 * a) for a in range(2)]
+        for a in range(2):
+            nc.sync.dma_start(out=w1_raw[a][:], in_=w1_rows[a])
 
         w3_rows = w3.rearrange("(p i) r -> p i r", i=4)
         w3_raw = [place("w3_raw%d" % b, [P, 4, 512], F32, 72 + 8 * b) for b in range(2)]
@@ -89,7 +92,8 @@ def tile_list_vanilla_bundle_ledger_kernel(
             nc.sync.dma_start(out=w3_raw[b][:], in_=w3_rows[:, :, 512 * b : 512 * (b + 1)])
 
         wgs_rows = wgs.rearrange("(q t) j -> q t j", t=4)
-        wg = [keep("wg%d" % t, [P, S], F32) for t in range(4)]
+        wg = [keep("wg%d" % t, [P, S], F32) for t in range(2)]
+        wg = wg + [place("wg2", [P, S], F32, 100), place("wg3", [P, S], F32, 96)]
 
         def load_wg(t, cols):
             for q in (0, 2, 1, 3):
@@ -114,10 +118,10 @@ def tile_list_vanilla_bundle_ledger_kernel(
         nc.sync.dma_start(list2[:], offs2)
         load_page(0)
         load_wg(0, slice(512, S))
-        nc.sync.dma_start(list3[:], offs3)
-        nc.sync.dma_start(list4[:], offs4)
         load_wg(1, slice(0, S))
         load_page(1)
+        nc.sync.dma_start(list3[:], offs3)
+        nc.sync.dma_start(list4[:], offs4)
         gs_sb = load_gain("gs_sb", gs)
         gx_sb = load_gain("gx_sb", gx)
         load_wg(2, slice(0, S))
@@ -132,11 +136,6 @@ def tile_list_vanilla_bundle_ledger_kernel(
         )
         load_page(4)
         gf_sb = load_gain("gf_sb", gf)
-        for q in range(4):
-            nc.sync.dma_start(
-                out=s4_raw[32 * q : 32 * q + 8, :].bitcast(I32),
-                in_=w4_scales[:, 4 * q : 4 * q + 4, :].bitcast(I32),
-            )
         for i in range(5, 8):
             load_page(i)
 
@@ -150,10 +149,15 @@ def tile_list_vanilla_bundle_ledger_kernel(
             out=w2_w[:].bitcast(U16).rearrange("p a (u c) -> p a u c", u=4),
             in_=w2_raw[:].bitcast(U16).rearrange("p a (c u) -> p a u c", u=4),
         )
-        w2_s = place("w2_s", [P, 2, R], U8, 12)
+        w2_s = keep("w2_s", [P, 2, R], U8)
         nc.vector.tensor_copy(
             out=w2_s[:].rearrange("p a (u c) -> p a u c", u=4),
             in_=s2_raw[:].rearrange("p a (c u) -> p a u c", u=4),
+        )
+        w4_s = place("w4_s", [P, H], U8, 104)
+        nc.vector.tensor_copy(
+            out=w4_s[:].rearrange("p (b u c) -> p b u c", b=2, u=4),
+            in_=s4_raw[:].rearrange("p (b c u) -> p b u c", b=2, u=4),
         )
         for g in range(4):
             nc.vector.tensor_copy(v_w[1][:, 256 * g : 256 * (g + 1)], tab_w[1][:].indirect(list1[:, 16 * g : 16 * (g + 1)]))
@@ -189,17 +193,12 @@ def tile_list_vanilla_bundle_ledger_kernel(
         def quantize(words, scales, values):
             nc.vector.quantize_mx(out=words.bitcast(FP8X4), scales=scales, in_=values)
 
-        nc.vector.tensor_copy(
-            out=w1_bf[0][:].rearrange("p u c i -> p c u i"),
-            in_=w1_raw0[:].rearrange("p i (c u) -> p c u i", u=4),
-        )
-        quantize(w1_w[:, 0, :], w1_s[:, 0, :], w1_bf[0][:].rearrange("p u c i -> p (u c i)"))
-        for e in range(2):
+        for a in range(2):
             nc.vector.tensor_copy(
-                out=w1_bf[1][:, :, 64 * e : 64 * (e + 1), :].rearrange("p u c i -> p c u i"),
-                in_=w1_raw1[e][:].rearrange("p i (c u) -> p c u i", u=4),
+                out=w1_bf[a][:].rearrange("p u c i -> p c u i"),
+                in_=w1_raw[a][:].rearrange("p i (c u) -> p c u i", u=4),
             )
-        quantize(w1_w[:, 1, :], w1_s[:, 1, :], w1_bf[1][:].rearrange("p u c i -> p (u c i)"))
+            quantize(w1_w[:, a, :], w1_s[:, a, :], w1_bf[a][:].rearrange("p u c i -> p (u c i)"))
 
         low_bf = [place("low_bf%d" % e, [P, 512, 4], BF16, 32 + 4 * e) for e in range(2)]
         low_w = keep("low_w", [P, S], U32)
@@ -257,15 +256,11 @@ def tile_list_vanilla_bundle_ledger_kernel(
                 in_=w4_raw[:, a, :].rearrange("p (b c u) -> p b c u", b=2, u=4),
             )
 
-        w4_s = keep("w4_s", [P, H], U8)
-        nc.vector.tensor_copy(
-            out=w4_s[:].rearrange("p (b u c) -> p b u c", b=2, u=4),
-            in_=s4_raw[:].rearrange("p (b c u) -> p b u c", b=2, u=4),
-        )
         x_bf = [place("x_bf%d" % b, [P, PICK, 4], BF16, 88 + 4 * b) for b in range(2)]
-        x_w = keep("x_w", [P, 2, PICK], U32)
+        x_w = [place("x_w0", [P, PICK], U32, 102), keep("x_w1", [P, PICK], U32)]
         x_s = keep("x_s", [P, 2, PICK], U8)
-        z_at = [32, 34, 36, 38, 28, 30, 92, 94]
+        z_at = [8, 10, 32, 96, 28, 30, 92, 94]
+        picked_at = [8, 10, 72, 24, 26, 100, 74, 72]
         z = {}
         y = {}
 
@@ -282,42 +277,60 @@ def tile_list_vanilla_bundle_ledger_kernel(
                     out=y[i][:],
                     lhsT=w4_w[:, a, rows].bitcast(FP8X4),
                     lhsT_scale=w4_s[4 * a : P, rows],
-                    rhs=x_w[:, a, :].bitcast(FP8X4),
+                    rhs=x_w[a][:].bitcast(FP8X4),
                     rhs_scale=x_s[:, a, :],
                     start=(a == 0),
                     stop=(a == 1),
                 )
 
-        for i in range(8):
-            b, t = divmod(i, 4)
+        def put_entries(i):
             pieces = 2 if i == 0 else 1
             n = S // pieces
             for e in range(pieces):
                 cols = slice(n * e, n * (e + 1))
                 nc.vector.tensor_tensor(
                     page[i][:].indirect(list2[:, n // 16 * e : n // 16 * (e + 1)]),
-                    h_sb[i][:, cols], wg[t][:, cols], ALU.mult,
+                    h_sb[i][:, cols], wg[i % 4][:, cols], ALU.mult,
                 )
-            picked = place("picked%d" % i, [P, PICK], F32, 72 + 2 * (i % 4))
+
+        def reread(i):
+            b, t = divmod(i, 4)
+            picked = place("picked%d" % i, [P, PICK], F32, picked_at[i])
             nc.vector.tensor_copy(picked[:], page[i][:].indirect(list3[:]))
-            bent = place("bent%d" % i, [P, PICK], F32, 80 + 2 * (i % 4))
+            bent = place("bent%d" % i, [P, PICK], F32, 76 + 2 * (i % 2))
             nc.scalar.activation(bent[:], picked[:], ACT.Tanh, scale=gs_sb[:, i : i + 1])
             nc.scalar.activation(x_bf[b][:, :, t], bent[:], ACT.Copy, scale=gx_sb[:, i : i + 1])
-            if i < 4:
-                fetch_finished(i)
-            if i == 7:
-                fetch_finished(4)
-                fetch_finished(5)
-            if t == 3:
-                quantize(x_w[:, b, :], x_s[:, b, :], x_bf[b][:].rearrange("p n t -> p (n t)"))
-                second_stage(b)
+
+        def close_pass(b):
+            quantize(x_w[b][:], x_s[:, b, :], x_bf[b][:].rearrange("p n t -> p (n t)"))
+            second_stage(b)
+
+        for group in ((0, 1, 2), (3, 4, 5, 6), (7,)):
+            for i in group:
+                put_entries(i)
+            for i in group:
+                reread(i)
+            if group[0] == 0:
+                for i in group:
+                    fetch_finished(i)
+            if group[0] == 3:
+                close_pass(0)
+        for i in (3, 4, 5):
+            fetch_finished(i)
+        close_pass(1)
         fetch_finished(6)
         fetch_finished(7)
 
         out_rows = out.rearrange("(b p t) j -> b t p j", b=2, t=4)
         for i in range(8):
             diff = place("diff%d" % i, [P, PICK], F32, 40 + 2 * (i % 4))
-            nc.vector.scalar_tensor_tensor(diff[:], z[i][:], gf_sb[:, i : i + 1], y[i][:], ALU.mult, ALU.subtract)
             res = place("res%d" % i, [P, PICK], F32, 48 + 2 * i)
-            nc.scalar.activation(res[:], diff[:], ACT.Tanh, scale=-1.0)
-            nc.sync.dma_start(out=out_rows[i // 4][i % 4], in_=res[:])
+            pieces = 2 if i == 7 else 1
+            n = PICK // pieces
+            for e in range(pieces):
+                cols = slice(n * e, n * (e + 1))
+                nc.vector.scalar_tensor_tensor(
+                    diff[:, cols], z[i][:, cols], gf_sb[:, i : i + 1], y[i][:, cols], ALU.mult, ALU.subtract
+                )
+                nc.scalar.activation(res[:, cols], diff[:, cols], ACT.Tanh, scale=-1.0)
+                nc.sync.dma_start(out=out_rows[i // 4][i % 4][:, cols], in_=res[:, cols])

from contextlib import ExitStack

import concourse.mybir as mybir

F32 = mybir.dt.float32
BF16 = mybir.dt.bfloat16
I32 = mybir.dt.int32
U32 = mybir.dt.uint32
U16 = mybir.dt.uint16
U8 = mybir.dt.uint8
FP8X4 = mybir.dt.float8_e4m3fn_x4
FP4X4 = mybir.dt.float4_e2m1fn_x4
ALU = mybir.AluOpType
ACT = mybir.ActivationFunctionType

K, R, H, T, S, T2, PICK = 1024, 512, 1024, 4096, 1024, 2048, 512
FLOPS = 2 * (2 * K * R * S + R * H * S + H * H * PICK)

P = 128
KB = 1024


def tile_list_vanilla_bundle_ledger_kernel(
    tc, tab_words, tab_scales, offs, w1, w2_words, w2_scales, w3, page0, wgs,
    offs2, offs3, offs4, gs, gx, w4_words, w4_scales, gf, out,
):
    nc = tc.nc
    with ExitStack() as ctx:
        held = ctx.enter_context(tc.tile_pool(name="held", bufs=1))
        arena = ctx.enter_context(tc.tile_pool(name="arena", bufs=1))
        psum = ctx.enter_context(tc.psum_pool(name="psum", bufs=1))

        def keep(name, shape, dtype):
            return held.tile(shape, dtype, name=name, align_bytes=64)

        def place(name, shape, dtype, kib):
            return arena.tile(shape, dtype, name=name, align_bytes=64, offset=kib * KB)

        def bank(i):
            return psum.tile([P, 512], F32, name="bank%d" % (i % 8))

        list1 = keep("list1", [P, S // 16], U16)
        list2 = keep("list2", [P, S // 16], U16)
        list3 = keep("list3", [P, PICK // 16], U16)
        list4 = keep("list4", [P, PICK // 16], U16)
        tab_w = [place("tab_w%d" % a, [P, T], U32, 16 * a) for a in range(2)]
        tab_s = place("tab_s", [P, T], U8, 104)
        v_s = [keep("v_s%d" % a, [P, S], U8) for a in range(2)]
        s2_raw = keep("s2_raw", [P, 2, R], U8)
        s4_raw = keep("s4_raw", [P, H], U8)

        nc.vector.memset(tab_s[:].bitcast(I32), 0)
        nc.gpsimd.memset(s2_raw[:].rearrange("p a c -> p (a c)").bitcast(I32), 0)
        nc.vector.memset(s4_raw[:].bitcast(I32), 0)
        nc.vector.memset(v_s[1][:].bitcast(I32), 0)

        for q in range(4):
            nc.gpsimd.dma_start(
                out=s2_raw[32 * q : 32 * q + 4, :, :].bitcast(I32),
                in_=w2_scales[:, 4 * q : 4 * q + 4, :].bitcast(I32).rearrange("a r c -> r a c"),
            )
        for q in range(4):
            nc.gpsimd.dma_start(
                out=s4_raw[32 * q : 32 * q + 8, :].bitcast(I32),
                in_=w4_scales[:, 4 * q : 4 * q + 4, :].bitcast(I32),
            )

        def load_table(a, first, last, n):
            words = tab_words[a].rearrange("p n i -> p (n i)").bitcast(I32)
            for c in range(first, last, n):
                nc.sync.dma_start(out=tab_w[a][:, c : c + n].bitcast(I32), in_=words[:, c : c + n])

        nc.sync.dma_start(list1[:], offs)
        load_table(0, 0, T - 512, 512)
        tab_rows = tab_scales.bitcast(I32).rearrange("a (q r) n -> r q a n", r=4)
        for r in range(4):
            nc.sync.dma_start(out=tab_s[r:P:16, :].bitcast(I32), in_=tab_rows[r])
        load_table(0, T - 512, T, 512)
        w2_raw = keep("w2_raw", [P, 2, 2 * R], U8)
        nc.sync.dma_start(out=w2_raw[:].bitcast(I32), in_=w2_words.bitcast(I32).rearrange("a p c -> p a c"))
        load_table(1, 0, T, T)

        w1_rows = w1.rearrange("(a p i) m -> a p i m", a=2, i=4)
        w1_raw = [place("w1_raw%d" % a, [P, 4, R], F32, 32 + 8 * a) for a in range(2)]
        for a in range(2):
            nc.sync.dma_start(out=w1_raw[a][:], in_=w1_rows[a])

        w3_rows = w3.rearrange("(p i) r -> p i r", i=4)
        w3_raw = [place("w3_raw%d" % b, [P, 4, 512], F32, 72 + 8 * b) for b in range(2)]

        def load_w3(b):
            nc.sync.dma_start(out=w3_raw[b][:], in_=w3_rows[:, :, 512 * b : 512 * (b + 1)])

        wgs_rows = wgs.rearrange("(q t) j -> q t j", t=4)
        wg = [keep("wg%d" % t, [P, S], F32) for t in range(2)]
        wg = wg + [place("wg2", [P, S], F32, 100), place("wg3", [P, S], F32, 96)]

        def load_wg(t, cols):
            for q in (0, 2, 1, 3):
                nc.sync.dma_start(out=wg[t][32 * q : 32 * q + 32, cols], in_=wgs_rows[:, t, cols])

        page_rows = page0.rearrange("(b p t) c -> b t p c", b=2, t=4)
        page = [keep("page%d" % i, [P, T2], F32) for i in range(8)]

        def load_page(i):
            nc.sync.dma_start(out=page[i][:], in_=page_rows[i // 4][i % 4])

        def load_gain(name, vec):
            tile = keep(name, [P, 8], F32)
            nc.sync.dma_start(
                out=tile[:].rearrange("p (b t) -> p b t", t=4),
                in_=vec.rearrange("(b p t) -> p b t", b=2, t=4),
            )
            return tile

        load_w3(0)
        load_wg(0, slice(0, 512))
        nc.sync.dma_start(list2[:], offs2)
        load_page(0)
        load_wg(0, slice(512, S))
        load_wg(1, slice(0, S))
        load_page(1)
        nc.sync.dma_start(list3[:], offs3)
        nc.sync.dma_start(list4[:], offs4)
        gs_sb = load_gain("gs_sb", gs)
        gx_sb = load_gain("gx_sb", gx)
        load_wg(2, slice(0, S))
        load_page(2)
        load_w3(1)
        load_wg(3, slice(0, S))
        load_page(3)
        w4_raw = keep("w4_raw", [P, 2, H], U32)
        nc.sync.dma_start(
            out=w4_raw[:].bitcast(I32),
            in_=w4_words.rearrange("a p c i -> p a (c i)").bitcast(I32),
        )
        load_page(4)
        gf_sb = load_gain("gf_sb", gf)
        for i in range(5, 8):
            load_page(i)

        nc.vector.tensor_copy(v_s[0][:], tab_s[:].indirect(list1[:]))
        nc.gpsimd.dma_start(out=v_s[1][0:112, :].bitcast(I32), in_=v_s[0][16:128, :].bitcast(I32))
        v_w = [keep("v_w%d" % a, [P, S], U32) for a in range(2)]
        nc.vector.tensor_copy(v_w[0][:], tab_w[0][:].indirect(list1[:]))

        w2_w = keep("w2_w", [P, 2, 2 * R], U8)
        nc.scalar.copy(
            out=w2_w[:].bitcast(U16).rearrange("p a (u c) -> p a u c", u=4),
            in_=w2_raw[:].bitcast(U16).rearrange("p a (c u) -> p a u c", u=4),
        )
        w2_s = keep("w2_s", [P, 2, R], U8)
        nc.vector.tensor_copy(
            out=w2_s[:].rearrange("p a (u c) -> p a u c", u=4),
            in_=s2_raw[:].rearrange("p a (c u) -> p a u c", u=4),
        )
        w4_s = place("w4_s", [P, H], U8, 104)
        nc.vector.tensor_copy(
            out=w4_s[:].rearrange("p (b u c) -> p b u c", b=2, u=4),
            in_=s4_raw[:].rearrange("p (b c u) -> p b u c", b=2, u=4),
        )
        for g in range(4):
            nc.vector.tensor_copy(v_w[1][:, 256 * g : 256 * (g + 1)], tab_w[1][:].indirect(list1[:, 16 * g : 16 * (g + 1)]))

        def first_stage(acc, c, words, scales):
            cols = slice(128 * c, 128 * (c + 1))
            for a in range(2):
                for u in range(4):
                    nc.tensor.matmul_mx(
                        out=acc[:, 128 * u : 128 * (u + 1)],
                        lhsT=words(a, u),
                        lhsT_scale=scales(a, u),
                        rhs=v_w[a][:, cols].bitcast(FP8X4),
                        rhs_scale=v_s[a][:, cols],
                        start=(a == 0 and u == 0),
                        stop=(a == 1 and u == 3),
                    )

        b_sb = [place("b_sb%d" % c, [P, 128, 4], F32, 48 + 2 * c) for c in range(8)]
        for c in range(8):
            acc = bank(c)
            first_stage(
                acc, c,
                lambda a, u: w2_w[:, a, 256 * u : 256 * (u + 1)].bitcast(FP4X4),
                lambda a, u: w2_s[:, a, 128 * u : 128 * (u + 1)],
            )
            nc.scalar.copy(out=b_sb[c][:], in_=acc[:].rearrange("p (u n) -> p n u", u=4))

        w1_bf = [place("w1_bf%d" % a, [P, 4, 128, 4], BF16, 64 + 4 * a) for a in range(2)]
        w1_w = keep("w1_w", [P, 2, R], U32)
        w1_s = keep("w1_s", [P, 2, R], U8)

        def quantize(words, scales, values):
            nc.vector.quantize_mx(out=words.bitcast(FP8X4), scales=scales, in_=values)

        for a in range(2):
            nc.vector.tensor_copy(
                out=w1_bf[a][:].rearrange("p u c i -> p c u i"),
                in_=w1_raw[a][:].rearrange("p i (c u) -> p c u i", u=4),
            )
            quantize(w1_w[:, a, :], w1_s[:, a, :], w1_bf[a][:].rearrange("p u c i -> p (u c i)"))

        low_bf = [place("low_bf%d" % e, [P, 512, 4], BF16, 32 + 4 * e) for e in range(2)]
        low_w = keep("low_w", [P, S], U32)
        low_s = keep("low_s", [P, S], U8)
        w3_bf = [place("w3_bf%d" % b, [P, 4, 128, 4], BF16, 88 + 4 * b) for b in range(2)]
        w3_w = keep("w3_w", [P, H], U32)
        w3_s = keep("w3_s", [P, H], U8)

        def prepare_w3(b):
            nc.scalar.copy(
                out=w3_bf[b][:].rearrange("p u c i -> p c u i"),
                in_=w3_raw[b][:].rearrange("p i (c u) -> p c u i", u=4),
            )
            cols = slice(512 * b, 512 * (b + 1))
            quantize(w3_w[:, cols], w3_s[:, cols], w3_bf[b][:].rearrange("p u c i -> p (u c i)"))

        prepare_w3(0)
        for c in range(8):
            acc = bank(c)
            first_stage(
                acc, c,
                lambda a, u: w1_w[:, a, 128 * u : 128 * (u + 1)].bitcast(FP8X4),
                lambda a, u: w1_s[:, a, 128 * u : 128 * (u + 1)],
            )
            e, n0 = c // 4, 128 * (c % 4)
            nc.vector.tensor_tensor(
                low_bf[e][:, n0 : n0 + 128, :], acc[:].rearrange("p (u n) -> p n u", u=4), b_sb[c][:], ALU.min
            )
            if c % 4 == 3:
                cols = slice(512 * e, 512 * (e + 1))
                quantize(low_w[:, cols], low_s[:, cols], low_bf[e][:].rearrange("p n u -> p (n u)"))
        prepare_w3(1)

        h_sb = [place("h_sb%d" % i, [P, S], F32, 4 * i) for i in range(8)]
        for i in range(8):
            rows = slice(128 * i, 128 * (i + 1))
            for e in range(2):
                cols = slice(512 * e, 512 * (e + 1))
                acc = bank(2 * i + e)
                nc.tensor.matmul_mx(
                    out=acc[:],
                    lhsT=w3_w[:, rows].bitcast(FP8X4),
                    lhsT_scale=w3_s[:, rows],
                    rhs=low_w[:, cols].bitcast(FP8X4),
                    rhs_scale=low_s[:, cols],
                    start=True,
                    stop=True,
                )
                nc.scalar.copy(out=h_sb[i][:, cols], in_=acc[:])

        w4_w = place("w4_w", [P, 2, H], U32, 64)
        for a in range(2):
            nc.scalar.copy(
                out=w4_w[:, a, :].rearrange("p (b u c) -> p b c u", b=2, u=4),
                in_=w4_raw[:, a, :].rearrange("p (b c u) -> p b c u", b=2, u=4),
            )

        x_bf = [place("x_bf%d" % b, [P, PICK, 4], BF16, 88 + 4 * b) for b in range(2)]
        x_w = [place("x_w0", [P, PICK], U32, 102), keep("x_w1", [P, PICK], U32)]
        x_s = keep("x_s", [P, 2, PICK], U8)
        z_at = [8, 10, 32, 96, 28, 30, 92, 94]
        picked_at = [8, 10, 72, 24, 26, 100, 74, 72]
        z = {}
        y = {}

        def fetch_finished(i):
            z[i] = place("z%d" % i, [P, PICK], F32, z_at[i])
            nc.vector.tensor_copy(z[i][:], page[i][:].indirect(list4[:]))

        def second_stage(a):
            for i in range(8):
                if a == 0:
                    y[i] = bank(i)
                rows = slice(128 * i, 128 * (i + 1))
                nc.tensor.matmul_mx(
                    out=y[i][:],
                    lhsT=w4_w[:, a, rows].bitcast(FP8X4),
                    lhsT_scale=w4_s[4 * a : P, rows],
                    rhs=x_w[a][:].bitcast(FP8X4),
                    rhs_scale=x_s[:, a, :],
                    start=(a == 0),
                    stop=(a == 1),
                )

        def put_entries(i):
            pieces = 2 if i == 0 else 1
            n = S // pieces
            for e in range(pieces):
                cols = slice(n * e, n * (e + 1))
                nc.vector.tensor_tensor(
                    page[i][:].indirect(list2[:, n // 16 * e : n // 16 * (e + 1)]),
                    h_sb[i][:, cols], wg[i % 4][:, cols], ALU.mult,
                )

        def reread(i):
            b, t = divmod(i, 4)
            picked = place("picked%d" % i, [P, PICK], F32, picked_at[i])
            nc.vector.tensor_copy(picked[:], page[i][:].indirect(list3[:]))
            bent = place("bent%d" % i, [P, PICK], F32, 76 + 2 * (i % 2))
            nc.scalar.activation(bent[:], picked[:], ACT.Tanh, scale=gs_sb[:, i : i + 1])
            nc.scalar.activation(x_bf[b][:, :, t], bent[:], ACT.Copy, scale=gx_sb[:, i : i + 1])

        def close_pass(b):
            quantize(x_w[b][:], x_s[:, b, :], x_bf[b][:].rearrange("p n t -> p (n t)"))
            second_stage(b)

        for group in ((0, 1, 2), (3, 4, 5, 6), (7,)):
            for i in group:
                put_entries(i)
            for i in group:
                reread(i)
            if group[0] == 0:
                for i in group:
                    fetch_finished(i)
            if group[0] == 3:
                close_pass(0)
        for i in (3, 4, 5):
            fetch_finished(i)
        close_pass(1)
        fetch_finished(6)
        fetch_finished(7)

        out_rows = out.rearrange("(b p t) j -> b t p j", b=2, t=4)
        for i in range(8):
            diff = place("diff%d" % i, [P, PICK], F32, 40 + 2 * (i % 4))
            res = place("res%d" % i, [P, PICK], F32, 48 + 2 * i)
            pieces = 2 if i == 7 else 1
            n = PICK // pieces
            for e in range(pieces):
                cols = slice(n * e, n * (e + 1))
                nc.vector.scalar_tensor_tensor(
                    diff[:, cols], z[i][:, cols], gf_sb[:, i : i + 1], y[i][:, cols], ALU.mult, ALU.subtract
                )
                nc.scalar.activation(res[:, cols], diff[:, cols], ACT.Tanh, scale=-1.0)
                nc.sync.dma_start(out=out_rows[i // 4][i % 4][:, cols], in_=res[:, cols])
